import numpy as np, ml_dtypes
CORES = [3,7,11,15,131,135,139,143]
N = 8
import mx_ref
BF = ml_dtypes.bfloat16
def cols(t, e):
    v = np.concatenate([t.reshape(128, -1, 4), np.zeros((128, 1, 4), BF)], axis=1)
    return np.ascontiguousarray(v[:, e]).reshape(128, -1)
def f(rng, *shape):
    return mx_ref.flush((rng.standard_normal(shape, dtype=np.float32) * np.exp2(rng.integers(-2, 3, shape[:-1] + (1,)))).astype(BF))
def wide(rng, *shape, cols=0):
    v = rng.standard_normal(shape, dtype=np.float32) * np.exp2(rng.integers(-12, 13, shape)).astype(np.float32)
    if cols: v *= np.repeat(np.exp2(rng.integers(-cols, cols + 1, shape[:-2] + (1, shape[-1] // 4))) * (rng.random(shape[:-2] + (1, shape[-1] // 4)) > 0.0625), 4, axis=-1).astype(np.float32)
    return mx_ref.flush(v.astype(BF))
T, NBIT, K, O = 96, 7, 128, 2
def planes(rng):
    v = np.zeros((N, 128, 512), BF); v[:, :, :4 * NBIT] = f(rng, N, 128, 4 * NBIT); return v
def setup_inputs(rng):
    return {"x": f(rng, N, 128, 4 * T), "hp": planes(rng), "e": f(rng, N, 128, 4 * K), "qw": f(rng, N, 128, O * 512)}
def setup_inputs_zero(rng):
    d = setup_inputs(rng)
    for r in rng.permutation(N)[:N // 2]:
        i = rng.integers(0, NBIT); d["hp"][r, :, 4 * i:4 * i + 4] = 0
    for r in range(N):
        for j in rng.permutation(T)[:T // 8]: d["x"][r, :, 4 * j:4 * j + 4] = 0
    return d
def setup_inputs_onebucket(rng):
    d = setup_inputs(rng); d["x"] = np.tile(d["hp"][rng.integers(0, N)][:, :4], (N, 1, T)); return d
def setup_inputs_all(rng):
    d = setup_inputs(rng); g = f(rng, 128, 4).astype(np.float32)[None, :, None, :]
    d["hp"][:, :, :4 * NBIT] = (g * np.exp2(rng.integers(0, 4, (N, 1, NBIT, 1)))).reshape(N, 128, -1).astype(BF)
    s = np.stack([rng.permutation(T) % 2 * 2 - 1 for r in range(N)]) * np.exp2(rng.integers(0, 4, (N, T)))
    d["x"] = (g * s[:, None, :, None]).reshape(N, 128, -1).astype(BF); return d
def setup_inputs_small(rng):
    d = setup_inputs(rng)
    for k in ("x", "hp"):
        v = d[k].astype(np.float32) * np.float32(2.0 ** -24)
        d[k] = mx_ref.flush(np.where(np.abs(v) < np.float32(2.0 ** -30), np.float32(0), v).astype(BF))
    return d
def setup_inputs_spread(rng):
    d = setup_inputs(rng); d["x"] = wide(rng, N, 128, 4 * T, cols=8); d["e"] = wide(rng, N, 128, 4 * K, cols=8); return d
def check_inputs(d):
    b = []
    if (np.asarray(d["hp"]).astype(np.float32)[:, :, 4 * NBIT:] != 0).any(): b.append("hp")
    return b
def reference(x, hp, e, qw):
    X = [mx_ref.quantize(x[r]) for r in range(N)]
    H = [mx_ref.quantize(hp[q]) for q in range(N)]
    W = [[mx_ref.quantize(np.ascontiguousarray(qw[r][:, 512 * o:512 * o + 512])) for o in range(O)] for r in range(N)]
    y = np.zeros((N, 128, N * O * T), np.float32); bk = np.zeros((N, N, T), np.float32)
    for r in range(N):
        for q in range(N):
            s = mx_ref.matmul(H[q], X[r])
            b = np.zeros(T, int)
            for i in range(NBIT): b += 2 ** i * (s[i] > 0)
            bk[r, q] = b
            c = mx_ref.quantize(cols(e[q], b))
            for o in range(O):
                k = (q * O + o) * T
                y[r][:, k:k + T] = mx_ref.matmul(W[r][o], c)
    return {"y": y, "bk": bk}

@@ -1,0 +1,217 @@
+import math
+from concourse.bass import DstId, RemoteDMATransfer
+from concourse.mybir import dt, AluOpType, ActivationFunctionType
+
+T_TOK, NBIT, K, O, N = 96, 7, 128, 2, 8
+G = 16
+A = T_TOK // G
+SL = 8
+Z = 128
+RUN = K + SL
+TA = SL
+HA = TA + K
+ZZ = HA + SL
+HB = ZZ + Z
+TB = HB + SL
+PITCH = 416
+NH = SL + Z + SL
+HBANKS, TBANKS = 4, 4
+
+SCRATCH = {
+    "eb": ("sbuf", [128, 4 * (ZZ + Z)], "bfloat16"),
+    "xs": ("sbuf", [128, A, 4 * G], "bfloat16"),
+    "xr": ("sbuf", [128, A, 512], "bfloat16"),
+    "qb": ("sbuf", [128, O * 512], "bfloat16"),
+    "ec": ("sbuf", [128, 4 * PITCH], "float8_e4m3fn_x4"),
+    "es": ("sbuf", [128, 4 * PITCH], "uint8"),
+    "xc": ("sbuf", [128, A * 128], "float8_e4m3fn_x4"),
+    "xp": ("sbuf", [128, A * 128], "uint8"),
+    "qc": ("sbuf", [128, O * 128], "float8_e4m3fn_x4"),
+    "qp": ("sbuf", [128, O * 128], "uint8"),
+    "bits": ("sbuf", [128, 4 * 128], "bfloat16"),
+    "half": ("sbuf", [128, 128], "bfloat16"),
+    "bsum": ("sbuf", [128, 4 * 128], "float32"),
+    "offs": ("sbuf", [128, 4 * 16], "uint16"),
+    "bt": ("sbuf", [128, 64], "float32"),
+    "prod": ("sbuf", [128, N * O * K], "float32"),
+    "ys": ("sbuf", [128, N * O * T_TOK], "float32"),
+    "hps": ("psum", [128, 512 * HBANKS], "float32"),
+    "tps": ("psum", [128, 512 * TBANKS], "float32"),
+}
+SEMAPHORES = ["le", "lh", "lx", "lq", "v", "s", "t", "ap", "a1", "a2", "a3", "sent", "st", "sst"]
+
+
+def rank_program(g, core, T, topo):
+    rank = T.rank_of(core)
+    if rank is None:
+        return
+    sem = T.sem
+    who = {}
+    for d in T.cores:
+        if d == core:
+            continue
+        same = topo.die(d) == topo.die(core)
+        if d in topo.cores_of(core):
+            who["partner"] = d
+        elif topo.mates(core, d):
+            who["mate_a" if same else "mate_b"] = d
+        elif topo.same_plane(core, d):
+            who["plane" if same else "plane_o"] = d
+        else:
+            who["diag" if same else "diag_o"] = d
+    pairs = [(core, who["partner"]), (who["plane"], who["diag"]), (who["mate_a"], who["mate_b"]), (who["plane_o"], who["diag_o"])]
+    qs = [(T.rank_of(a), T.rank_of(b)) for a, b in pairs]
+
+    cnt = {"v": 0, "s": 0, "t": 0}
+
+    def inc(call, name):
+        call.then_inc(sem[name], 1)
+        cnt[name] += 1
+        return cnt[name]
+
+    V, S, PE, Y = g.vector, g.scalar, g.tensor, g.sync
+    COPY = ActivationFunctionType.Copy
+
+    S.dma_start(T.eb[:, 0:4 * SL], T.hp[:, 0:4 * SL]).then_inc(sem.lh, 16)
+    S.dma_start(T.eb[:, 4 * HA:4 * ZZ], T.hp[:, 0:4 * SL]).then_inc(sem.lh, 16)
+    Y.dma_start(T.eb[:, 4 * TA:4 * HA], T.e[:]).then_inc(sem.le, 16)
+    Y.dma_start(T.xs[:], T.x[:]).then_inc(sem.lx, 16)
+    Y.dma_start(T.qb[:], T.qw[:]).then_inc(sem.lq, 16)
+
+    inc(V.memset(T.eb[:, 4 * ZZ:4 * (ZZ + Z)], 0.0), "v")
+    inc(V.memset(T.bits[:], 0.0), "v")
+    m = inc(V.memset(T.half[:], 0.5), "v")
+    V.wait_ge(sem.v, m)
+    inc(V.memset(T.half[:, 0:128:8], 0.0), "v")
+
+    V.wait_ge(sem.le, 16)
+    V.wait_ge(sem.lh, 32)
+    own = inc(V.quantize_mx(T.ec[:, 0:ZZ], T.es[:, 0:ZZ], T.eb[:, 0:4 * ZZ]), "v")
+    V.wait_ge(sem.v, 4)
+    for k in range(4):
+        z = k * PITCH + ZZ
+        inc(V.quantize_mx(T.ec[:, z:z + Z], T.es[:, z:z + Z], T.eb[:, 4 * ZZ:4 * (ZZ + Z)]), "v")
+
+    def cores_mask(es):
+        return sum(1 << e for e in es)
+
+    def fused(items, codes):
+        tr = []
+        for d, es, c0, c1, s in items:
+            rid, pid = topo.addr(d, core)
+            buf = T.ec if codes else T.es
+            src, dst = buf[:, c0:c0 + RUN], buf[:, c1:c1 + RUN]
+            if codes:
+                src, dst = src.bitcast(dt.uint8), dst.bitcast(dt.uint8)
+            tr.append(RemoteDMATransfer(dst_ids=[DstId(rid=rid, pnc=pid)], dma_engine_mask=cores_mask(es), remote_sem=s, src=src, dst=dst))
+        g.remote_dma_fused(tr, local_sem=sem.sent)
+        return sum(len(es) for d, es, c0, c1, s in items)
+
+    far = topo.engines(core, who["diag"])
+    near = topo.engines(core, who["partner"])
+    h = len(far) // 2
+    inner = [e for e in near if e not in far]
+    n1 = len(near) // 2
+    first = [(who["plane"], far[:h], TA, PITCH + TA, sem.a1), (who["diag"], far[h:], 0, PITCH + HB, sem.a1)]
+    second = [(who["mate_a"], far[:h], TA, 2 * PITCH + TA, sem.a2), (who["mate_b"], far[h:], 0, 2 * PITCH + HB, sem.a2),
+              (who["partner"], inner, 0, HB, sem.ap)]
+    relay = [(who["partner"], near[:n1], PITCH + TA, 3 * PITCH + TA, sem.a3), (who["partner"], near[n1:], PITCH + HB, 3 * PITCH + HB, sem.a3)]
+    sent = 0
+    g.wait_ge(sem.v, own)
+    for items in (first, second):
+        sent += fused(items, True)
+        sent += fused(items, False)
+    all1 = 2 * len(far)
+    g.wait_ge(sem.a1, all1)
+    sent += fused(relay, True)
+    sent += fused(relay, False)
+
+    V.wait_ge(sem.lx, 16)
+    S.wait_ge(sem.lx, 16)
+    for i in range(8):
+        o_, i_ = T.xr[:, :, 4 * G * i:4 * G * (i + 1)], T.xs[:, :, :]
+        if i < 5:
+            vx = inc(V.tensor_copy(o_, i_), "v")
+        else:
+            sx = inc(S.activation(o_, i_, COPY), "s")
+    V.wait_ge(sem.v, vx)
+    V.wait_ge(sem.s, sx)
+    for a in range(A):
+        inc(V.quantize_mx(T.xc[:, 128 * a:128 * (a + 1)], T.xp[:, 128 * a:128 * (a + 1)], T.xr[:, a, :]), "v")
+    V.wait_ge(sem.lq, 16)
+    ready = inc(V.quantize_mx(T.qc[:], T.qp[:], T.qb[:]), "v")
+
+    arrived = [(sem.ap, 2 * len(inner)), (sem.a1, all1), (sem.a2, 2 * len(far)), (sem.a3, 2 * len(near))]
+    hfree, tfree = [0] * HBANKS, [0] * TBANKS
+    PE.wait_ge(sem.v, ready)
+    nst = nsst = 0
+    for k in range(4):
+        base = k * PITCH
+        PE.wait_ge(arrived[k][0], arrived[k][1])
+        for a in range(A):
+            b = a % HBANKS
+            if hfree[b]:
+                PE.wait_ge(sem.v, hfree[b])
+            c = base + HA
+            t = inc(PE.matmul_mx(T.hps[:, 512 * b:512 * b + NH], T.xc[:, 128 * a:128 * (a + 1)], T.xp[:, 128 * a:128 * (a + 1)],
+                                 T.ec[:, c:c + NH], T.es[:, c:c + NH], True, True), "t")
+            V.wait_ge(sem.t, t)
+            for slot in range(2):
+                d, s = 128 * k + 64 * slot + 8 * a, 512 * b + slot * (SL + Z)
+                hfree[b] = inc(V.tensor_scalar(T.bits[:, d:d + NBIT], T.hps[:, s:s + NBIT], 0.0, float(2 ** (NBIT - 1)),
+                                               AluOpType.is_gt, AluOpType.mult), "v")
+        pc = []
+        for slot in range(2):
+            for o in range(O):
+                i = slot * O + o
+                c = base + (TB if slot else TA)
+                if tfree[i]:
+                    PE.wait_ge(sem.s, tfree[i])
+                t = inc(PE.matmul_mx(T.tps[:, 512 * i:512 * i + K], T.qc[:, 128 * o:128 * (o + 1)], T.qp[:, 128 * o:128 * (o + 1)],
+                                     T.ec[:, c:c + K], T.es[:, c:c + K], True, True), "t")
+                S.wait_ge(sem.t, t)
+                w = (qs[k][slot] * O + o) * K
+                tfree[i] = inc(S.activation(T.prod[:, w:w + K], T.tps[:, 512 * i:512 * i + K], COPY), "s")
+                pc.append(tfree[i])
+        V.wait_ge(sem.v, cnt["v"])
+        n = inc(V.tensor_tensor_scan(T.bsum[:, 128 * k:128 * (k + 1)], T.half[:], T.bits[:, 128 * k:128 * (k + 1)], 0.0,
+                                     AluOpType.mult, AluOpType.add), "v")
+        V.wait_ge(sem.v, n)
+        lists = inc(V.tensor_copy(T.offs[:, 16 * k:16 * (k + 1)], T.bsum[:, 128 * k + NBIT - 1:128 * (k + 1):8]), "v")
+        V.wait_ge(sem.v, lists)
+        V.wait_ge(sem.s, pc[O - 1])
+        S.wait_ge(sem.v, lists)
+        S.wait_ge(sem.s, pc[2 * O - 1])
+        for slot in range(2):
+            for o in range(O):
+                j = qs[k][slot] * O + o
+                out, win = T.ys[:, T_TOK * j:T_TOK * (j + 1)], T.prod[:, K * j:K * (j + 1)]
+                lst = T.offs[:, 16 * k + 8 * slot:16 * k + 8 * slot + A]
+                if slot == 0:
+                    gv = inc(V.tensor_copy(out, win.indirect(lst)), "v")
+                else:
+                    gs = inc(S.activation(out, win.indirect(lst), COPY), "s")
+        if k % 2:
+            b = k // 2
+            tr = inc(V.transpose(T.bt[0:32, 32 * b:32 * (b + 1)], T.bsum[0:32, 256 * b + NBIT - 1:256 * (b + 1):8]), "v")
+        wy = O * T_TOK
+        qa, qb = qs[k]
+        Y.wait_ge(sem.v, gv)
+        Y.dma_start(T.y[:, wy * qa:wy * (qa + 1)], T.ys[:, wy * qa:wy * (qa + 1)]).then_inc(sem.st, 16)
+        S.wait_ge(sem.s, gs)
+        S.dma_start(T.y[:, wy * qb:wy * (qb + 1)], T.ys[:, wy * qb:wy * (qb + 1)]).then_inc(sem.sst, 16)
+        nst += 16
+        nsst += 16
+        if k % 2:
+            Y.wait_ge(sem.v, tr)
+            for i in range(4):
+                q = qs[2 * b + i // 2][i % 2]
+                Y.dma_start(T.bk[q:q + 1, :], T.bt[8 * i:8 * i + A, 32 * b:32 * b + G]).then_inc(sem.st, 16)
+                nst += 16
+
+    g.wait_ge(sem.sent, sent)
+    g.wait_ge(sem.v, cnt["v"])
+    g.wait_ge(sem.s, cnt["s"])
+    g.wait_ge(sem.t, cnt["t"])
+    S.wait_ge(sem.sst, nsst)
+    Y.wait_ge(sem.st, nst)

@@ -6,47 +6,93 @@ T_TOK, NBIT, K, O, N = 96, 7, 128, 2, 8
 G = 16
 A = T_TOK // G
 SL = 8
-Z = 128
 RUN = K + SL
-TA = SL
-HA = TA + K
+NH = 128
+O0 = 8
+OP = O0 + RUN
+TP = OP + NH
+TA, HA = 0, K
 ZZ = HA + SL
-HB = ZZ + Z
-TB = HB + SL
-PITCH = 416
-NH = SL + Z + SL
+BASE = (O0 + SL, TP + RUN, TP + RUN + 2 * RUN + NH)
+ZEROS = (NH - SL, NH, NH - 2 * SL)
+HB = tuple(ZZ + z for z in ZEROS)
+TB = tuple(b + SL for b in HB)
+TO1 = BASE[2] + TB[2] + K
+TO2 = TO1 + K
+COLS = TO2 + K
 HBANKS, TBANKS = 4, 4
+HE = 8
 
 SCRATCH = {
-    "eb": ("sbuf", [128, 4 * (ZZ + Z)], "bfloat16"),
+    "hb": ("sbuf", [128, 4 * (SL + NH)], "bfloat16"),
+    "eb": ("sbuf", [128, 4 * RUN], "bfloat16"),
     "xs": ("sbuf", [128, A, 4 * G], "bfloat16"),
     "xr": ("sbuf", [128, A, 512], "bfloat16"),
     "qb": ("sbuf", [128, O * 512], "bfloat16"),
-    "ec": ("sbuf", [128, 4 * PITCH], "float8_e4m3fn_x4"),
-    "es": ("sbuf", [128, 4 * PITCH], "uint8"),
+    "ec": ("sbuf", [128, COLS], "float8_e4m3fn_x4"),
+    "es": ("sbuf", [128, COLS], "uint8"),
     "xc": ("sbuf", [128, A * 128], "float8_e4m3fn_x4"),
     "xp": ("sbuf", [128, A * 128], "uint8"),
     "qc": ("sbuf", [128, O * 128], "float8_e4m3fn_x4"),
     "qp": ("sbuf", [128, O * 128], "uint8"),
-    "bits": ("sbuf", [128, 4 * 128], "bfloat16"),
-    "half": ("sbuf", [128, 128], "bfloat16"),
-    "bsum": ("sbuf", [128, 4 * 128], "float32"),
-    "offs": ("sbuf", [128, 4 * 16], "uint16"),
+    "bits": ("sbuf", [128, N * 64], "bfloat16"),
+    "half": ("sbuf", [128, 256], "bfloat16"),
+    "bsum": ("sbuf", [128, N * 64], "float32"),
+    "offs": ("sbuf", [128, N * 8], "uint16"),
     "bt": ("sbuf", [128, 64], "float32"),
     "prod": ("sbuf", [128, N * O * K], "float32"),
     "ys": ("sbuf", [128, N * O * T_TOK], "float32"),
     "hps": ("psum", [128, 512 * HBANKS], "float32"),
     "tps": ("psum", [128, 512 * TBANKS], "float32"),
 }
-SEMAPHORES = ["le", "lh", "lx", "lq", "v", "s", "t", "ap", "a1", "a2", "a3", "sent", "st", "sst"]
+SEMAPHORES = ["le", "lh", "lx", "lq", "v", "s", "t", "ah", "hc", "hs", "ap", "a1c", "a1s", "a2", "a3", "z", "sent", "st", "sst"]
+
+
+def send(g, core, T, topo, items, n, codes):
+    tr = []
+    for d, es, c0, c1, s in items:
+        rid, pid = topo.addr(d, core)
+        buf = T.ec if codes else T.es
+        src, dst = buf[:, c0:c0 + n], buf[:, c1:c1 + n]
+        if codes:
+            src, dst = src.bitcast(dt.uint8), dst.bitcast(dt.uint8)
+        tr.append(RemoteDMATransfer(dst_ids=[DstId(rid=rid, pnc=pid)], dma_engine_mask=sum(1 << e for e in es), remote_sem=s, src=src, dst=dst))
+    g.remote_dma_fused(tr, local_sem=T.sem.sent)
+    return sum(len(i[1]) for i in items)
+
+
+def helper_program(g, core, dests, T, topo):
+    items = []
+    for d in dests:
+        es = topo.engines(core, d)
+        n = len(es) // 2
+        if topo.same_plane(core, d):
+            items.append((d, es[:n], 0, BASE[2] + ZZ, T.sem.ah))
+        else:
+            items.append((d, es[n:], 0, BASE[2] + ZZ + SL, T.sem.ah))
+    sent = 0
+    for codes, s in ((True, T.sem.hc), (False, T.sem.hs)):
+        g.wait_ge(s, HE)
+        sent += send(g, core, T, topo, items, SL, codes)
+    g.wait_ge(T.sem.sent, sent)
 
 
 def rank_program(g, core, T, topo):
+    sem = T.sem
+    helper = None
+    for r in T.cores:
+        if core not in topo.cores_of(r):
+            continue
+        dests = [d for d in T.cores if topo.die(d) != topo.die(r) and d not in topo.cores_of(r) and not topo.mates(r, d)]
+        spare = [c for c in topo.cores_of(r) if c not in T.cores and topo.die(c) == topo.die(r) and all(topo.may_write(c, d) for d in dests)]
+        if core == spare[0]:
+            helper_program(g, core, dests, T, topo)
+        if core == r:
+            helper = spare[0]
     rank = T.rank_of(core)
     if rank is None:
         return
-    sem = T.sem
-    who = {}
+    who = {"own": core}
     for d in T.cores:
         if d == core:
             continue
@@ -59,8 +105,7 @@ def rank_program(g, core, T, topo):
             who["plane" if same else "plane_o"] = d
         else:
             who["diag" if same else "diag_o"] = d
-    pairs = [(core, who["partner"]), (who["plane"], who["diag"]), (who["mate_a"], who["mate_b"]), (who["plane_o"], who["diag_o"])]
-    qs = [(T.rank_of(a), T.rank_of(b)) for a, b in pairs]
+    q_of = {n: T.rank_of(d) for n, d in who.items()}
 
     cnt = {"v": 0, "s": 0, "t": 0}
 
@@ -72,59 +117,64 @@ def rank_program(g, core, T, topo):
     V, S, PE, Y = g.vector, g.scalar, g.tensor, g.sync
     COPY = ActivationFunctionType.Copy
 
-    S.dma_start(T.eb[:, 0:4 * SL], T.hp[:, 0:4 * SL]).then_inc(sem.lh, 16)
-    S.dma_start(T.eb[:, 4 * HA:4 * ZZ], T.hp[:, 0:4 * SL]).then_inc(sem.lh, 16)
-    Y.dma_start(T.eb[:, 4 * TA:4 * HA], T.e[:]).then_inc(sem.le, 16)
+    S.dma_start(T.hb[:, 0:4 * SL], T.hp[:, 0:4 * SL]).then_inc(sem.lh, 16)
+    Y.dma_start(T.eb[:, 4 * SL:4 * RUN], T.e[:]).then_inc(sem.le, 16)
     Y.dma_start(T.xs[:], T.x[:]).then_inc(sem.lx, 16)
     Y.dma_start(T.qb[:], T.qw[:]).then_inc(sem.lq, 16)
 
-    inc(V.memset(T.eb[:, 4 * ZZ:4 * (ZZ + Z)], 0.0), "v")
-    inc(V.memset(T.bits[:], 0.0), "v")
+    inc(V.memset(T.hb[:, 4 * SL:4 * (SL + NH)], 0.0), "v")
     m = inc(V.memset(T.half[:], 0.5), "v")
+    inc(V.memset(T.bits[:], 0.0), "v")
     V.wait_ge(sem.v, m)
-    inc(V.memset(T.half[:, 0:128:8], 0.0), "v")
-
+    inc(V.memset(T.half[:, 0:256:8], 0.0), "v")
+    V.wait_ge(sem.v, cnt["v"])
+    V.wait_ge(sem.lh, 16)
+    hq = inc(V.quantize_mx(T.ec[:, OP:TP], T.es[:, OP:TP], T.hb[:, 0:4 * NH]), "v")
+    n = inc(V.tensor_copy(T.eb[:, 0:4 * SL], T.hb[:, 0:4 * SL]), "v")
+    V.wait_ge(sem.v, n)
     V.wait_ge(sem.le, 16)
-    V.wait_ge(sem.lh, 32)
-    own = inc(V.quantize_mx(T.ec[:, 0:ZZ], T.es[:, 0:ZZ], T.eb[:, 0:4 * ZZ]), "v")
-    V.wait_ge(sem.v, 4)
-    for k in range(4):
-        z = k * PITCH + ZZ
-        inc(V.quantize_mx(T.ec[:, z:z + Z], T.es[:, z:z + Z], T.eb[:, 4 * ZZ:4 * (ZZ + Z)]), "v")
+    own = inc(V.quantize_mx(T.ec[:, O0:OP], T.es[:, O0:OP], T.eb[:]), "v")
+    z1 = BASE[1] + ZZ
+    inc(V.quantize_mx(T.ec[:, z1:z1 + NH], T.es[:, z1:z1 + NH], T.hb[:, 4 * SL:4 * (SL + NH)]), "v")
 
-    def cores_mask(es):
-        return sum(1 << e for e in es)
-
-    def fused(items, codes):
-        tr = []
-        for d, es, c0, c1, s in items:
-            rid, pid = topo.addr(d, core)
-            buf = T.ec if codes else T.es
-            src, dst = buf[:, c0:c0 + RUN], buf[:, c1:c1 + RUN]
-            if codes:
-                src, dst = src.bitcast(dt.uint8), dst.bitcast(dt.uint8)
-            tr.append(RemoteDMATransfer(dst_ids=[DstId(rid=rid, pnc=pid)], dma_engine_mask=cores_mask(es), remote_sem=s, src=src, dst=dst))
-        g.remote_dma_fused(tr, local_sem=sem.sent)
-        return sum(len(es) for d, es, c0, c1, s in items)
+    c0, c1, w = OP + SL, BASE[2] + ZZ + 2 * SL, ZEROS[2] - 2 * SL
+    Y.wait_ge(sem.v, hq)
+    Y.dma_start(T.ec[:, c1:c1 + w].bitcast(dt.uint8), T.ec[:, c0:c0 + w].bitcast(dt.uint8)).then_inc(sem.z, 16)
+    Y.dma_start(T.es[:, c1:c1 + w], T.es[:, c0:c0 + w]).then_inc(sem.z, 16)
 
     far = topo.engines(core, who["diag"])
     near = topo.engines(core, who["partner"])
-    h = len(far) // 2
     inner = [e for e in near if e not in far]
-    n1 = len(near) // 2
-    first = [(who["plane"], far[:h], TA, PITCH + TA, sem.a1), (who["diag"], far[h:], 0, PITCH + HB, sem.a1)]
-    second = [(who["mate_a"], far[:h], TA, 2 * PITCH + TA, sem.a2), (who["mate_b"], far[h:], 0, 2 * PITCH + HB, sem.a2),
-              (who["partner"], inner, 0, HB, sem.ap)]
-    relay = [(who["partner"], near[:n1], PITCH + TA, 3 * PITCH + TA, sem.a3), (who["partner"], near[n1:], PITCH + HB, 3 * PITCH + HB, sem.a3)]
-    sent = 0
+    h = len(far) // 2
+    hi = len(inner) // 2
+
+    def early(s):
+        return [(helper, inner[:HE], OP, 0, s)]
+
+    def first(s):
+        return [(who["plane"], far[:h], O0 + SL, BASE[1] + TA, s), (who["diag"], far[h:], O0, BASE[1] + HB[1], s),
+                (who["partner"], inner, O0, TP, sem.ap)]
+
+    second = [(who["mate_a"], far[:h], O0 + SL, BASE[2] + TA, sem.a2), (who["mate_b"], far[h:], O0, BASE[2] + HB[2], sem.a2)]
+
+    def relay(e1, e2):
+        return [(who["partner"], e1, BASE[1] + TA, TO1, sem.a3), (who["partner"], e2, BASE[1] + TB[1], TO2, sem.a3)]
+
+    def snd(items, n, codes):
+        return send(g, core, T, topo, items, n, codes)
+
+    g.wait_ge(sem.v, hq)
+    sent = snd(early(sem.hc), SL, True)
     g.wait_ge(sem.v, own)
-    for items in (first, second):
-        sent += fused(items, True)
-        sent += fused(items, False)
-    all1 = 2 * len(far)
-    g.wait_ge(sem.a1, all1)
-    sent += fused(relay, True)
-    sent += fused(relay, False)
+    sent += snd(first(sem.a1c), RUN, True)
+    sent += snd(early(sem.hs), SL, False)
+    sent += snd(first(sem.a1s), RUN, False)
+    sent += snd(second, RUN, True)
+    sent += snd(second, RUN, False)
+    g.wait_ge(sem.a1c, len(far))
+    sent += snd(relay(inner[:hi], inner[hi:]), K, True)
+    g.wait_ge(sem.a1s, len(far))
+    sent += snd(relay(far, inner), K, False)
 
     V.wait_ge(sem.lx, 16)
     S.wait_ge(sem.lx, 16)
@@ -139,79 +189,113 @@ def rank_program(g, core, T, topo):
     for a in range(A):
         inc(V.quantize_mx(T.xc[:, 128 * a:128 * (a + 1)], T.xp[:, 128 * a:128 * (a + 1)], T.xr[:, a, :]), "v")
     V.wait_ge(sem.lq, 16)
-    ready = inc(V.quantize_mx(T.qc[:], T.qp[:], T.qb[:]), "v")
+    qq = inc(V.quantize_mx(T.qc[:], T.qp[:], T.qb[:]), "v")
 
-    arrived = [(sem.ap, 2 * len(inner)), (sem.a1, all1), (sem.a2, 2 * len(far)), (sem.a3, 2 * len(near))]
-    hfree, tfree = [0] * HBANKS, [0] * TBANKS
-    PE.wait_ge(sem.v, ready)
-    nst = nsst = 0
-    for k in range(4):
-        base = k * PITCH
-        PE.wait_ge(arrived[k][0], arrived[k][1])
+    hfree, tfree, nt = [0] * HBANKS, [None] * TBANKS, [0]
+
+    def hashes(p, runs):
+        c, nh = BASE[p] + HA, 2 * SL + ZEROS[p]
         for a in range(A):
             b = a % HBANKS
             if hfree[b]:
                 PE.wait_ge(sem.v, hfree[b])
-            c = base + HA
-            t = inc(PE.matmul_mx(T.hps[:, 512 * b:512 * b + NH], T.xc[:, 128 * a:128 * (a + 1)], T.xp[:, 128 * a:128 * (a + 1)],
-                                 T.ec[:, c:c + NH], T.es[:, c:c + NH], True, True), "t")
+            t = inc(PE.matmul_mx(T.hps[:, 512 * b:512 * b + nh], T.xc[:, 128 * a:128 * (a + 1)], T.xp[:, 128 * a:128 * (a + 1)],
+                                 T.ec[:, c:c + nh], T.es[:, c:c + nh], True, True), "t")
             V.wait_ge(sem.t, t)
-            for slot in range(2):
-                d, s = 128 * k + 64 * slot + 8 * a, 512 * b + slot * (SL + Z)
-                hfree[b] = inc(V.tensor_scalar(T.bits[:, d:d + NBIT], T.hps[:, s:s + NBIT], 0.0, float(2 ** (NBIT - 1)),
+            for c0, ks in runs:
+                w = SL * len(ks)
+                d, s = 64 * ks[0] + w * a, 512 * b + c0
+                hfree[b] = inc(V.tensor_scalar(T.bits[:, d:d + w - 1], T.hps[:, s:s + w - 1], 0.0, float(2 ** (NBIT - 1)),
                                                AluOpType.is_gt, AluOpType.mult), "v")
-        pc = []
-        for slot in range(2):
-            for o in range(O):
-                i = slot * O + o
-                c = base + (TB if slot else TA)
-                if tfree[i]:
-                    PE.wait_ge(sem.s, tfree[i])
-                t = inc(PE.matmul_mx(T.tps[:, 512 * i:512 * i + K], T.qc[:, 128 * o:128 * (o + 1)], T.qp[:, 128 * o:128 * (o + 1)],
-                                     T.ec[:, c:c + K], T.es[:, c:c + K], True, True), "t")
-                S.wait_ge(sem.t, t)
-                w = (qs[k][slot] * O + o) * K
-                tfree[i] = inc(S.activation(T.prod[:, w:w + K], T.tps[:, 512 * i:512 * i + K], COPY), "s")
-                pc.append(tfree[i])
+        ks = sorted(k for c0, l in runs for k in l)
+        lo, hi_ = 64 * ks[0], 64 * (ks[-1] + 1)
         V.wait_ge(sem.v, cnt["v"])
-        n = inc(V.tensor_tensor_scan(T.bsum[:, 128 * k:128 * (k + 1)], T.half[:], T.bits[:, 128 * k:128 * (k + 1)], 0.0,
-                                     AluOpType.mult, AluOpType.add), "v")
+        n = inc(V.tensor_tensor_scan(T.bsum[:, lo:hi_], T.half[:, 0:hi_ - lo], T.bits[:, lo:hi_], 0.0, AluOpType.mult, AluOpType.add), "v")
         V.wait_ge(sem.v, n)
-        lists = inc(V.tensor_copy(T.offs[:, 16 * k:16 * (k + 1)], T.bsum[:, 128 * k + NBIT - 1:128 * (k + 1):8]), "v")
-        V.wait_ge(sem.v, lists)
-        V.wait_ge(sem.s, pc[O - 1])
-        S.wait_ge(sem.v, lists)
-        S.wait_ge(sem.s, pc[2 * O - 1])
-        for slot in range(2):
-            for o in range(O):
-                j = qs[k][slot] * O + o
-                out, win = T.ys[:, T_TOK * j:T_TOK * (j + 1)], T.prod[:, K * j:K * (j + 1)]
-                lst = T.offs[:, 16 * k + 8 * slot:16 * k + 8 * slot + A]
-                if slot == 0:
-                    gv = inc(V.tensor_copy(out, win.indirect(lst)), "v")
-                else:
-                    gs = inc(S.activation(out, win.indirect(lst), COPY), "s")
-        if k % 2:
-            b = k // 2
-            tr = inc(V.transpose(T.bt[0:32, 32 * b:32 * (b + 1)], T.bsum[0:32, 256 * b + NBIT - 1:256 * (b + 1):8]), "v")
-        wy = O * T_TOK
-        qa, qb = qs[k]
-        Y.wait_ge(sem.v, gv)
-        Y.dma_start(T.y[:, wy * qa:wy * (qa + 1)], T.ys[:, wy * qa:wy * (qa + 1)]).then_inc(sem.st, 16)
-        S.wait_ge(sem.s, gs)
-        S.dma_start(T.y[:, wy * qb:wy * (qb + 1)], T.ys[:, wy * qb:wy * (qb + 1)]).then_inc(sem.sst, 16)
-        nst += 16
-        nsst += 16
-        if k % 2:
-            Y.wait_ge(sem.v, tr)
-            for i in range(4):
-                q = qs[2 * b + i // 2][i % 2]
-                Y.dma_start(T.bk[q:q + 1, :], T.bt[8 * i:8 * i + A, 32 * b:32 * b + G]).then_inc(sem.st, 16)
-                nst += 16
+        if all(len(l) == 1 for c0, l in runs):
+            return inc(V.tensor_copy(T.offs[:, 8 * ks[0]:8 * (ks[-1] + 1)], T.bsum[:, lo + NBIT - 1:hi_:8]), "v")
+        for c0, l in runs:
+            w = SL * len(l)
+            for i, k in enumerate(l):
+                f = 64 * l[0] + SL * i + NBIT - 1
+                r = inc(V.tensor_copy(T.offs[:, 8 * k:8 * k + A], T.bsum[:, f:64 * l[0] + A * w:w]), "v")
+        return r
+
+    ready = {}
+
+    def tables(c, name, on_vector=False):
+        for o in range(O):
+            i = nt[0] % TBANKS
+            nt[0] += 1
+            if tfree[i]:
+                PE.wait_ge(*tfree[i])
+            t = inc(PE.matmul_mx(T.tps[:, 512 * i:512 * i + K], T.qc[:, 128 * o:128 * (o + 1)], T.qp[:, 128 * o:128 * (o + 1)],
+                                 T.ec[:, c:c + K], T.es[:, c:c + K], True, True), "t")
+            E, n = (V, "v") if on_vector else (S, "s")
+            E.wait_ge(sem.t, t)
+            w = (q_of[name] * O + o) * K
+            out, in_ = T.prod[:, w:w + K], T.tps[:, 512 * i:512 * i + K]
+            tfree[i] = ready[name] = (sem[n], inc(V.tensor_copy(out, in_) if on_vector else S.activation(out, in_, COPY), n))
+
+    nst = {"st": 0, "sst": 0}
+
+    def pick(name, k, lists, on_vector):
+        q = q_of[name]
+        E, D, own_, dsem = (V, Y, "v", "st") if on_vector else (S, S, "s", "sst")
+        E.wait_ge(sem.v, lists)
+        E.wait_ge(*ready[name])
+        for o in range(O):
+            j = q * O + o
+            out, win = T.ys[:, T_TOK * j:T_TOK * (j + 1)], T.prod[:, K * j:K * (j + 1)].indirect(T.offs[:, 8 * k:8 * k + A])
+            n = inc(V.tensor_copy(out, win) if on_vector else S.activation(out, win, COPY), own_)
+        w = O * T_TOK
+        D.wait_ge(sem[own_], n)
+        D.dma_start(T.y[:, w * q:w * (q + 1)], T.ys[:, w * q:w * (q + 1)]).then_inc(sem[dsem], 16)
+        nst[dsem] += 16
+
+    def buckets(b, rows):
+        n = inc(V.transpose(T.bt[0:32, 32 * b:32 * (b + 1)], T.bsum[0:32, 256 * b + NBIT - 1:256 * (b + 1):8]), "v")
+        Y.wait_ge(sem.v, n)
+        for name, p, step in rows:
+            q = q_of[name]
+            Y.dma_start(T.bk[q:q + 1, :], T.bt[p:p + (A - 1) * step + 1:step, 32 * b:32 * b + G]).then_inc(sem.st, 16)
+            nst["st"] += 16
+
+    PE.wait_ge(sem.v, qq)
+    tables(BASE[0] + TA, "own")
+    PE.wait_ge(sem.ap, 2 * len(inner))
+    l0 = hashes(0, [(0, [0]), (SL + ZEROS[0], [1])])
+    tables(TP + SL, "partner")
+    pick("own", 0, l0, False)
+    pick("partner", 1, l0, False)
+
+    PE.wait_ge(sem.a1c, len(far))
+    PE.wait_ge(sem.a1s, len(far))
+    l1 = hashes(1, [(0, [2]), (SL + ZEROS[1], [3])])
+    tables(BASE[1] + TA, "plane")
+    tables(BASE[1] + TB[1], "diag")
+    pick("plane", 2, l1, True)
+    pick("diag", 3, l1, False)
+    buckets(0, [("own", 0, 1), ("partner", 8, 1), ("plane", 16, 1), ("diag", 24, 1)])
+
+    PE.wait_ge(sem.a2, 2 * len(far))
+    PE.wait_ge(sem.ah, 2 * len(far))
+    PE.wait_ge(sem.z, 32)
+    l2 = hashes(2, [(0, [4, 5, 6]), (SL + ZEROS[2], [7])])
+    tables(BASE[2] + TA, "mate_a")
+    tables(BASE[2] + TB[2], "mate_b")
+    pick("mate_a", 4, l2, True)
+    PE.wait_ge(sem.a3, 2 * len(inner) + len(far))
+    tables(TO1, "plane_o", True)
+    pick("mate_b", 7, l2, False)
+    tables(TO2, "diag_o")
+    pick("plane_o", 5, l2, True)
+    pick("diag_o", 6, l2, False)
+    buckets(1, [("mate_a", 0, 3), ("plane_o", 1, 3), ("diag_o", 2, 3), ("mate_b", 24, 1)])
 
     g.wait_ge(sem.sent, sent)
     g.wait_ge(sem.v, cnt["v"])
     g.wait_ge(sem.s, cnt["s"])
     g.wait_ge(sem.t, cnt["t"])
-    S.wait_ge(sem.sst, nsst)
-    Y.wait_ge(sem.st, nst)
+    S.wait_ge(sem.sst, nst["sst"])
+    Y.wait_ge(sem.st, nst["st"])

import math
from concourse.bass import DstId, RemoteDMATransfer
from concourse.mybir import dt, AluOpType, ActivationFunctionType

T_TOK, NBIT, K, O, N = 96, 7, 128, 2, 8
G = 16
A = T_TOK // G
SL = 8
RUN = K + SL
NH = 128
O0 = 8
OP = O0 + RUN
TP = OP + NH
TA, HA = 0, K
ZZ = HA + SL
BASE = (O0 + SL, TP + RUN, TP + RUN + 2 * RUN + NH)
ZEROS = (NH - SL, NH, NH - 2 * SL)
HB = tuple(ZZ + z for z in ZEROS)
TB = tuple(b + SL for b in HB)
TO1 = BASE[2] + TB[2] + K
TO2 = TO1 + K
COLS = TO2 + K
HBANKS, TBANKS = 4, 4
HE = 8

SCRATCH = {
    "hb": ("sbuf", [128, 4 * (SL + NH)], "bfloat16"),
    "eb": ("sbuf", [128, 4 * RUN], "bfloat16"),
    "xs": ("sbuf", [128, A, 4 * G], "bfloat16"),
    "xr": ("sbuf", [128, A, 512], "bfloat16"),
    "qb": ("sbuf", [128, O * 512], "bfloat16"),
    "ec": ("sbuf", [128, COLS], "float8_e4m3fn_x4"),
    "es": ("sbuf", [128, COLS], "uint8"),
    "xc": ("sbuf", [128, A * 128], "float8_e4m3fn_x4"),
    "xp": ("sbuf", [128, A * 128], "uint8"),
    "qc": ("sbuf", [128, O * 128], "float8_e4m3fn_x4"),
    "qp": ("sbuf", [128, O * 128], "uint8"),
    "bits": ("sbuf", [128, N * 64], "bfloat16"),
    "half": ("sbuf", [128, 256], "bfloat16"),
    "bsum": ("sbuf", [128, N * 64], "float32"),
    "offs": ("sbuf", [128, N * 8], "uint16"),
    "bt": ("sbuf", [128, 64], "float32"),
    "prod": ("sbuf", [128, N * O * K], "float32"),
    "ys": ("sbuf", [128, N * O * T_TOK], "float32"),
    "hps": ("psum", [128, 512 * HBANKS], "float32"),
    "tps": ("psum", [128, 512 * TBANKS], "float32"),
}
SEMAPHORES = ["le", "lh", "lx", "lq", "v", "s", "t", "ah", "hc", "hs", "ap", "a1c", "a1s", "a2", "a3", "z", "sent", "st", "sst"]


def send(g, core, T, topo, items, n, codes):
    tr = []
    for d, es, c0, c1, s in items:
        rid, pid = topo.addr(d, core)
        buf = T.ec if codes else T.es
        src, dst = buf[:, c0:c0 + n], buf[:, c1:c1 + n]
        if codes:
            src, dst = src.bitcast(dt.uint8), dst.bitcast(dt.uint8)
        tr.append(RemoteDMATransfer(dst_ids=[DstId(rid=rid, pnc=pid)], dma_engine_mask=sum(1 << e for e in es), remote_sem=s, src=src, dst=dst))
    g.remote_dma_fused(tr, local_sem=T.sem.sent)
    return sum(len(i[1]) for i in items)


def helper_program(g, core, dests, T, topo):
    items = []
    for d in dests:
        es = topo.engines(core, d)
        n = len(es) // 2
        if topo.same_plane(core, d):
            items.append((d, es[:n], 0, BASE[2] + ZZ, T.sem.ah))
        else:
            items.append((d, es[n:], 0, BASE[2] + ZZ + SL, T.sem.ah))
    sent = 0
    for codes, s in ((True, T.sem.hc), (False, T.sem.hs)):
        g.wait_ge(s, HE)
        sent += send(g, core, T, topo, items, SL, codes)
    g.wait_ge(T.sem.sent, sent)


def rank_program(g, core, T, topo):
    sem = T.sem
    helper = None
    for r in T.cores:
        if core not in topo.cores_of(r):
            continue
        dests = [d for d in T.cores if topo.die(d) != topo.die(r) and d not in topo.cores_of(r) and not topo.mates(r, d)]
        spare = [c for c in topo.cores_of(r) if c not in T.cores and topo.die(c) == topo.die(r) and all(topo.may_write(c, d) for d in dests)]
        if core == spare[0]:
            helper_program(g, core, dests, T, topo)
        if core == r:
            helper = spare[0]
    rank = T.rank_of(core)
    if rank is None:
        return
    who = {"own": core}
    for d in T.cores:
        if d == core:
            continue
        same = topo.die(d) == topo.die(core)
        if d in topo.cores_of(core):
            who["partner"] = d
        elif topo.mates(core, d):
            who["mate_a" if same else "mate_b"] = d
        elif topo.same_plane(core, d):
            who["plane" if same else "plane_o"] = d
        else:
            who["diag" if same else "diag_o"] = d
    q_of = {n: T.rank_of(d) for n, d in who.items()}

    cnt = {"v": 0, "s": 0, "t": 0}

    def inc(call, name):
        call.then_inc(sem[name], 1)
        cnt[name] += 1
        return cnt[name]

    V, S, PE, Y = g.vector, g.scalar, g.tensor, g.sync
    COPY = ActivationFunctionType.Copy

    S.dma_start(T.hb[:, 0:4 * SL], T.hp[:, 0:4 * SL]).then_inc(sem.lh, 16)
    Y.dma_start(T.eb[:, 4 * SL:4 * RUN], T.e[:]).then_inc(sem.le, 16)
    Y.dma_start(T.xs[:], T.x[:]).then_inc(sem.lx, 16)
    Y.dma_start(T.qb[:], T.qw[:]).then_inc(sem.lq, 16)

    inc(V.memset(T.hb[:, 4 * SL:4 * (SL + NH)], 0.0), "v")
    m = inc(V.memset(T.half[:], 0.5), "v")
    inc(V.memset(T.bits[:], 0.0), "v")
    V.wait_ge(sem.v, m)
    inc(V.memset(T.half[:, 0:256:8], 0.0), "v")
    V.wait_ge(sem.v, cnt["v"])
    V.wait_ge(sem.lh, 16)
    hq = inc(V.quantize_mx(T.ec[:, OP:TP], T.es[:, OP:TP], T.hb[:, 0:4 * NH]), "v")
    n = inc(V.tensor_copy(T.eb[:, 0:4 * SL], T.hb[:, 0:4 * SL]), "v")
    V.wait_ge(sem.v, n)
    V.wait_ge(sem.le, 16)
    own = inc(V.quantize_mx(T.ec[:, O0:OP], T.es[:, O0:OP], T.eb[:]), "v")
    z1 = BASE[1] + ZZ
    inc(V.quantize_mx(T.ec[:, z1:z1 + NH], T.es[:, z1:z1 + NH], T.hb[:, 4 * SL:4 * (SL + NH)]), "v")

    c0, c1, w = OP + SL, BASE[2] + ZZ + 2 * SL, ZEROS[2] - 2 * SL
    Y.wait_ge(sem.v, hq)
    Y.dma_start(T.ec[:, c1:c1 + w].bitcast(dt.uint8), T.ec[:, c0:c0 + w].bitcast(dt.uint8)).then_inc(sem.z, 16)
    Y.dma_start(T.es[:, c1:c1 + w], T.es[:, c0:c0 + w]).then_inc(sem.z, 16)

    far = topo.engines(core, who["diag"])
    near = topo.engines(core, who["partner"])
    inner = [e for e in near if e not in far]
    h = len(far) // 2
    hi = len(inner) // 2

    def early(s):
        return [(helper, inner[:HE], OP, 0, s)]

    def first(s):
        return [(who["plane"], far[:h], O0 + SL, BASE[1] + TA, s), (who["diag"], far[h:], O0, BASE[1] + HB[1], s),
                (who["partner"], inner, O0, TP, sem.ap)]

    second = [(who["mate_a"], far[:h], O0 + SL, BASE[2] + TA, sem.a2), (who["mate_b"], far[h:], O0, BASE[2] + HB[2], sem.a2)]

    def relay(e1, e2):
        return [(who["partner"], e1, BASE[1] + TA, TO1, sem.a3), (who["partner"], e2, BASE[1] + TB[1], TO2, sem.a3)]

    def snd(items, n, codes):
        return send(g, core, T, topo, items, n, codes)

    g.wait_ge(sem.v, hq)
    sent = snd(early(sem.hc), SL, True)
    g.wait_ge(sem.v, own)
    sent += snd(first(sem.a1c), RUN, True)
    sent += snd(early(sem.hs), SL, False)
    sent += snd(first(sem.a1s), RUN, False)
    sent += snd(second, RUN, True)
    sent += snd(second, RUN, False)
    g.wait_ge(sem.a1c, len(far))
    sent += snd(relay(inner[:hi], inner[hi:]), K, True)
    g.wait_ge(sem.a1s, len(far))
    sent += snd(relay(far, inner), K, False)

    V.wait_ge(sem.lx, 16)
    S.wait_ge(sem.lx, 16)
    for i in range(8):
        o_, i_ = T.xr[:, :, 4 * G * i:4 * G * (i + 1)], T.xs[:, :, :]
        if i < 5:
            vx = inc(V.tensor_copy(o_, i_), "v")
        else:
            sx = inc(S.activation(o_, i_, COPY), "s")
    V.wait_ge(sem.v, vx)
    V.wait_ge(sem.s, sx)
    for a in range(A):
        inc(V.quantize_mx(T.xc[:, 128 * a:128 * (a + 1)], T.xp[:, 128 * a:128 * (a + 1)], T.xr[:, a, :]), "v")
    V.wait_ge(sem.lq, 16)
    qq = inc(V.quantize_mx(T.qc[:], T.qp[:], T.qb[:]), "v")

    hfree, tfree, nt = [0] * HBANKS, [None] * TBANKS, [0]

    def hashes(p, runs):
        c, nh = BASE[p] + HA, 2 * SL + ZEROS[p]
        for a in range(A):
            b = a % HBANKS
            if hfree[b]:
                PE.wait_ge(sem.v, hfree[b])
            t = inc(PE.matmul_mx(T.hps[:, 512 * b:512 * b + nh], T.xc[:, 128 * a:128 * (a + 1)], T.xp[:, 128 * a:128 * (a + 1)],
                                 T.ec[:, c:c + nh], T.es[:, c:c + nh], True, True), "t")
            V.wait_ge(sem.t, t)
            for c0, ks in runs:
                w = SL * len(ks)
                d, s = 64 * ks[0] + w * a, 512 * b + c0
                hfree[b] = inc(V.tensor_scalar(T.bits[:, d:d + w - 1], T.hps[:, s:s + w - 1], 0.0, float(2 ** (NBIT - 1)),
                                               AluOpType.is_gt, AluOpType.mult), "v")
        ks = sorted(k for c0, l in runs for k in l)
        lo, hi_ = 64 * ks[0], 64 * (ks[-1] + 1)
        V.wait_ge(sem.v, cnt["v"])
        n = inc(V.tensor_tensor_scan(T.bsum[:, lo:hi_], T.half[:, 0:hi_ - lo], T.bits[:, lo:hi_], 0.0, AluOpType.mult, AluOpType.add), "v")
        V.wait_ge(sem.v, n)
        if all(len(l) == 1 for c0, l in runs):
            return inc(V.tensor_copy(T.offs[:, 8 * ks[0]:8 * (ks[-1] + 1)], T.bsum[:, lo + NBIT - 1:hi_:8]), "v")
        for c0, l in runs:
            w = SL * len(l)
            for i, k in enumerate(l):
                f = 64 * l[0] + SL * i + NBIT - 1
                r = inc(V.tensor_copy(T.offs[:, 8 * k:8 * k + A], T.bsum[:, f:64 * l[0] + A * w:w]), "v")
        return r

    ready = {}

    def tables(c, name, on_vector=False):
        for o in range(O):
            i = nt[0] % TBANKS
            nt[0] += 1
            if tfree[i]:
                PE.wait_ge(*tfree[i])
            t = inc(PE.matmul_mx(T.tps[:, 512 * i:512 * i + K], T.qc[:, 128 * o:128 * (o + 1)], T.qp[:, 128 * o:128 * (o + 1)],
                                 T.ec[:, c:c + K], T.es[:, c:c + K], True, True), "t")
            E, n = (V, "v") if on_vector else (S, "s")
            E.wait_ge(sem.t, t)
            w = (q_of[name] * O + o) * K
            out, in_ = T.prod[:, w:w + K], T.tps[:, 512 * i:512 * i + K]
            tfree[i] = ready[name] = (sem[n], inc(V.tensor_copy(out, in_) if on_vector else S.activation(out, in_, COPY), n))

    nst = {"st": 0, "sst": 0}

    def pick(name, k, lists, on_vector):
        q = q_of[name]
        E, D, own_, dsem = (V, Y, "v", "st") if on_vector else (S, S, "s", "sst")
        E.wait_ge(sem.v, lists)
        E.wait_ge(*ready[name])
        for o in range(O):
            j = q * O + o
            out, win = T.ys[:, T_TOK * j:T_TOK * (j + 1)], T.prod[:, K * j:K * (j + 1)].indirect(T.offs[:, 8 * k:8 * k + A])
            n = inc(V.tensor_copy(out, win) if on_vector else S.activation(out, win, COPY), own_)
        w = O * T_TOK
        D.wait_ge(sem[own_], n)
        D.dma_start(T.y[:, w * q:w * (q + 1)], T.ys[:, w * q:w * (q + 1)]).then_inc(sem[dsem], 16)
        nst[dsem] += 16

    def buckets(b, rows):
        n = inc(V.transpose(T.bt[0:32, 32 * b:32 * (b + 1)], T.bsum[0:32, 256 * b + NBIT - 1:256 * (b + 1):8]), "v")
        Y.wait_ge(sem.v, n)
        for name, p, step in rows:
            q = q_of[name]
            Y.dma_start(T.bk[q:q + 1, :], T.bt[p:p + (A - 1) * step + 1:step, 32 * b:32 * b + G]).then_inc(sem.st, 16)
            nst["st"] += 16

    PE.wait_ge(sem.v, qq)
    tables(BASE[0] + TA, "own")
    PE.wait_ge(sem.ap, 2 * len(inner))
    l0 = hashes(0, [(0, [0]), (SL + ZEROS[0], [1])])
    tables(TP + SL, "partner")
    pick("own", 0, l0, False)
    pick("partner", 1, l0, False)

    PE.wait_ge(sem.a1c, len(far))
    PE.wait_ge(sem.a1s, len(far))
    l1 = hashes(1, [(0, [2]), (SL + ZEROS[1], [3])])
    tables(BASE[1] + TA, "plane")
    tables(BASE[1] + TB[1], "diag")
    pick("plane", 2, l1, True)
    pick("diag", 3, l1, False)
    buckets(0, [("own", 0, 1), ("partner", 8, 1), ("plane", 16, 1), ("diag", 24, 1)])

    PE.wait_ge(sem.a2, 2 * len(far))
    PE.wait_ge(sem.ah, 2 * len(far))
    PE.wait_ge(sem.z, 32)
    l2 = hashes(2, [(0, [4, 5, 6]), (SL + ZEROS[2], [7])])
    tables(BASE[2] + TA, "mate_a")
    tables(BASE[2] + TB[2], "mate_b")
    pick("mate_a", 4, l2, True)
    PE.wait_ge(sem.a3, 2 * len(inner) + len(far))
    tables(TO1, "plane_o", True)
    pick("mate_b", 7, l2, False)
    tables(TO2, "diag_o")
    pick("plane_o", 5, l2, True)
    pick("diag_o", 6, l2, False)
    buckets(1, [("mate_a", 0, 3), ("plane_o", 1, 3), ("diag_o", 2, 3), ("mate_b", 24, 1)])

    g.wait_ge(sem.sent, sent)
    g.wait_ge(sem.v, cnt["v"])
    g.wait_ge(sem.s, cnt["s"])
    g.wait_ge(sem.t, cnt["t"])
    S.wait_ge(sem.sst, nst["sst"])
    Y.wait_ge(sem.st, nst["st"])
